import numpy as np
import ml_dtypes


def mxq(x, axis, fmt="e4m3"):
    dtype, down = {"e4m3": (ml_dtypes.float8_e4m3fn, 7), "e5m2": (ml_dtypes.float8_e5m2, 14)}[fmt]
    v = np.moveaxis(np.asarray(x, np.float32).astype(ml_dtypes.bfloat16).astype(np.float64), axis, -1)
    blocks = v.reshape(v.shape[:-1] + (-1, 32))
    amax = np.abs(blocks).max(-1, keepdims=True)
    byte = np.maximum(np.where(amax > 0, np.frexp(amax)[1] - 1 + 127, 0) - down, 1)
    scale = np.exp2(byte - 127.0)
    codes = (blocks / scale).astype(np.float32).astype(dtype).astype(np.float64)
    return np.moveaxis((codes * scale).reshape(v.shape), -1, axis)


WIDE = False


def mx_kscale(k):
    if not WIDE:
        return np.ones(k)
    levels = np.array([10, -10, 5, -5, 0])
    if k % 512:
        return np.exp2(np.random.permutation(np.resize(levels, k // 32))).repeat(32)
    a = np.empty((k // 512, 16))
    for p in range(k // 512):
        a[p, :8] = np.random.permutation(np.resize(levels, 8))
        for g in range(8):
            far = levels[np.abs(levels - a[p, g]) >= 10]
            a[p, g + 8] = far[np.random.randint(len(far))]
    return np.exp2(a.ravel()).repeat(32)


def f64(x):
    return np.asarray(x).astype(np.float64)


def striped(idx):
    return np.tile(idx.reshape(-1, 16).T, (8, 1)).astype(np.uint16)


def unstriped(offs):
    return offs[:16].T.reshape(-1).astype(np.int64)


def striped8(idx):
    return np.concatenate([x.reshape(-1, 16).T for x in idx]).astype(np.uint16)


def runs(offs, k):
    lists = np.stack([offs[16 * r : 16 * r + 16].T.reshape(-1) for r in range(8)]).astype(np.int64)
    return lists[np.arange(k) % 512 // 64]


def pack_weight(w):
    k, n = w.shape
    w = f64(np.asarray(w, np.float32).astype(ml_dtypes.bfloat16)).reshape(k // 32, 32, n)
    amax = np.abs(w).max(1)
    byte = np.clip(np.where(amax > 0, np.frexp(amax)[1] - 1 + 127 - 7, 1), 1, 254)
    scaled = (w * np.exp2(127.0 - byte)[:, None, :]).reshape(k, n).astype(np.float32)
    words = np.ascontiguousarray(scaled.reshape(k // 512, 128, 4, n).transpose(0, 1, 3, 2)).astype(ml_dtypes.float8_e4m3fn).view(np.uint8)
    return words, np.ascontiguousarray(byte.astype(np.uint8).reshape(k // 512, 16, n))


def unpack_weight(words, scales):
    g, p, n, _ = words.shape
    vals = np.ascontiguousarray(words).view(ml_dtypes.float8_e4m3fn).astype(np.float64) * np.repeat(np.exp2(scales.astype(np.float64) - 127.0), 8, axis=1)[..., None]
    return vals.transpose(0, 1, 3, 2).reshape(g * 512, n)


K, T, S, V, N, H = 512, 2048, 512, 256, 512, 512


def setup_inputs():
    n = np.random.standard_normal
    s = mx_kscale(K)[:, None]
    u = mx_kscale(H)
    packed_xT = pack_weight(n((K, T)) * s)
    perm = np.stack([np.random.permutation(S) for _ in range(8)])
    return {
        "x_words": packed_xT[0],
        "x_scales": packed_xT[1],
        "w1": (n((K, H)) / np.sqrt(K) / s).astype(np.float32),
        "gn": (np.random.uniform(0.5, 1.5, (H, 1)) * u[:, None]).astype(np.float32),
        "w2": (n((H, N)) / np.sqrt(H) / u[:, None]).astype(np.float32),
        "offs": striped(np.random.permutation(T)[:S]),
        "n1": striped8(np.stack([np.random.permutation(S) for _ in range(8)])),
        "la": striped8(perm[:, :V]),
        "lb": striped8(perm[:, V:]),
    }


def reference(x_words, x_scales, w1, gn, w2, offs, n1, la, lb):
    xq = unpack_weight(x_words, x_scales)[:, unstriped(offs)]
    y = mxq(f64(w1), 0, "e4m3").T @ xq
    a = y[np.arange(H)[:, None], runs(n1, H)]
    z = f64(gn) * ((y * a) / ((y) ** 2 + (a) ** 2 + 0.25))
    h = mxq(f64(w2), 0, "e4m3").T @ mxq(z, 0, "e4m3")
    c = h[np.arange(N)[:, None], runs(la, N)]
    d = h[np.arange(N)[:, None], runs(lb, N)]
    nb = np.minimum(c, d)
    na = np.maximum(c, d)
    p = np.zeros((N, S))
    p[np.arange(N)[:, None], runs(la, N)] = na
    out = p.copy()
    out[np.arange(N)[:, None], runs(lb, N)] = nb
    return out

@@ -1,0 +1,228 @@
+from contextlib import ExitStack
+
+import concourse.mybir as mybir
+
+K, T, S, V, N, H = 512, 2048, 512, 256, 512, 512
+FLOPS = 2 * K * H * S + 2 * H * N * S
+
+F32 = mybir.dt.float32
+BF16 = mybir.dt.bfloat16
+I32 = mybir.dt.int32
+U32 = mybir.dt.uint32
+U16 = mybir.dt.uint16
+U8 = mybir.dt.uint8
+FP8X4 = mybir.dt.float8_e4m3fn_x4
+ALU = mybir.AluOpType
+ACT = mybir.ActivationFunctionType
+
+P = 128
+PACK = 4
+UNITS = ((0, 256), (256, 128), (384, 128))
+
+
+def tile_picked_normord_none_p_kernel(tc, x_words, x_scales, w1, gn, w2, offs, n1, la, lb, out):
+    nc = tc.nc
+    with ExitStack() as ctx:
+        lists = ctx.enter_context(tc.tile_pool(name="lists", bufs=1))
+        keep = ctx.enter_context(tc.tile_pool(name="keep", bufs=1))
+        psum = ctx.enter_context(tc.psum_pool(name="psum", bufs=1))
+
+        offs_sb = lists.tile([P, S // 16], U16, name="offs_sb")
+        n1_sb = lists.tile([P, S // 16], U16, name="n1_sb")
+        la_sb = lists.tile([P, V // 16], U16, name="la_sb")
+        lb_sb = lists.tile([P, V // 16], U16, name="lb_sb")
+
+        xw = keep.tile([P, T], U32, name="xw", align_bytes=64)
+        xs = keep.tile([P, T], U8, name="xs", align_bytes=64)
+        nc.vector.memset(xs[:].bitcast(I32), 0)
+        one = keep.tile([P, 1], F32, name="one")
+        nc.vector.memset(one[:], 1.0)
+        warm = keep.tile([P, 1], F32, name="warm")
+        nc.scalar.activation(warm[:], one[:], ACT.Abs_reciprocal_sqrt)
+
+        nc.sync.dma_start(xw[:].bitcast(I32), x_words[0].rearrange("p n t -> p (n t)").bitcast(I32))
+        for q in range(4):
+            nc.sync.dma_start(xs[32 * q : 32 * q + 4, :].bitcast(I32), x_scales[0, 4 * q : 4 * q + 4, :].bitcast(I32))
+        nc.sync.dma_start(offs_sb[:], offs)
+        w1_rows = w1.rearrange("(p j) c -> p j c", j=PACK)
+        w1_raw = [keep.tile([P, PACK, H // 2], F32, name="w1_raw%d" % u) for u in range(2)]
+        for u in range(2):
+            nc.sync.dma_start(w1_raw[u][:], w1_rows[:, :, u * 256 : (u + 1) * 256])
+        nc.sync.dma_start(n1_sb[:], n1)
+        gn_sb = keep.tile([P, PACK], F32, name="gn_sb")
+        nc.sync.dma_start(gn_sb[:], gn.rearrange("(p t) o -> p (t o)", t=PACK))
+        w2_raw = keep.tile([P, PACK, N], F32, name="w2_raw")
+        nc.sync.dma_start(w2_raw[:], w2.rearrange("(p j) c -> p j c", j=PACK))
+        nc.sync.dma_start(la_sb[:], la)
+        nc.sync.dma_start(lb_sb[:], lb)
+
+        gw = keep.tile([P, S], U32, name="gw", align_bytes=64)
+        gs = keep.tile([P, S], U8, name="gs", align_bytes=64)
+        nc.vector.tensor_copy(gw[:], xw[:].indirect(offs_sb[:]))
+        nc.vector.tensor_copy(gs[:], xs[:].indirect(offs_sb[:]))
+
+        w1b = keep.tile([P, PACK, P, PACK], BF16, name="w1b", align_bytes=64)
+        w1_dst = w1b[:].rearrange("p t m j -> p m j t")
+        w1_src = [raw[:].rearrange("p j (m t) -> p m j t", t=PACK) for raw in w1_raw]
+        nc.scalar.copy(w1_dst[:, 0:64], w1_src[0])
+        nc.vector.tensor_copy(w1_dst[:, 64:104], w1_src[1][:, 0:40])
+        nc.scalar.copy(w1_dst[:, 104:128], w1_src[1][:, 40:64])
+
+        w1c = keep.tile([P, H], U32, name="w1c", align_bytes=64)
+        w1s = keep.tile([P, H], U8, name="w1s", align_bytes=64)
+        ybank = [psum.tile([P, S], F32, name="ybank%d" % t, tag="ybank%d" % t) for t in range(PACK)]
+        for t in range(PACK):
+            cols = slice(t * P, (t + 1) * P)
+            nc.vector.quantize_mx(out=w1c[:, cols].bitcast(FP8X4), scales=w1s[:, cols], in_=w1b[:, t].rearrange("p m j -> p (m j)"))
+        for t in range(PACK):
+            cols = slice(t * P, (t + 1) * P)
+            nc.tensor.matmul_mx(out=ybank[t][:], lhsT=w1c[:, cols].bitcast(FP8X4), lhsT_scale=w1s[:, cols],
+                                rhs=gw[:].bitcast(FP8X4), rhs_scale=gs[:], start=True, stop=True)
+        ys = [keep.tile([P, S], F32, name="ys%d" % t) for t in range(PACK)]
+        nc.vector.tensor_copy(ys[0][:], ybank[0][:])
+        for t in range(1, PACK):
+            nc.scalar.copy(ys[t][:], ybank[t][:])
+        y2 = [keep.tile([P, PACK, S // 2], F32, name="y2%d" % u) for u in range(2)]
+
+        def square_y(half):
+            for t in range(PACK):
+                nc.scalar.activation(y2[half][:, t, :], ybank[t][:, half * 256 : (half + 1) * 256], ACT.Square)
+
+        w2c = [keep.tile([P, 2 * P], U32, name="w2c%d" % u, align_bytes=64) for u in range(2)]
+        w2s = [keep.tile([P, 2 * P], U8, name="w2s%d" % u, align_bytes=64) for u in range(2)]
+        w2_src = w2_raw[:].rearrange("p j (m t) -> p m j t", t=PACK)
+        w2b = {}
+
+        def lay_w2(u, tag):
+            w2b[u] = keep.tile([P, 2, P, PACK], BF16, name="w2b%d" % u, tag=tag, align_bytes=64)
+            nc.scalar.copy(w2b[u][:].rearrange("p t m j -> p m j t"), w2_src[:, :, :, 2 * u : 2 * u + 2])
+
+        def quant_w2(u):
+            nc.vector.quantize_mx(out=w2c[u][:].bitcast(FP8X4), scales=w2s[u][:], in_=w2b[u][:].rearrange("p t m j -> p (t m j)"))
+
+        hbank = [psum.tile([P, S], F32, name="hbank%d" % t) for t in range(PACK)]
+        zc = keep.tile([P, S], U32, name="zc", align_bytes=64)
+        zs = keep.tile([P, S], U8, name="zs", align_bytes=64)
+        a, num, a2, den, r, r2, zb = {}, {}, {}, {}, {}, {}, {}
+
+        def fetch(half, tag):
+            a[half] = keep.tile([P, PACK, 256], F32, name="a%d" % half, tag=tag)
+            for t in range(PACK):
+                nc.vector.tensor_copy(a[half][:, t, :], ys[t][:].indirect(n1_sb[:, half * 16 : (half + 1) * 16]))
+
+        def numer(half):
+            num[half] = keep.tile([P, PACK, 256], F32, name="num%d" % half)
+            for t in range(PACK):
+                nc.vector.scalar_tensor_tensor(num[half][:, t, :], ybank[t][:, half * 256 : (half + 1) * 256], gn_sb[:, t : t + 1], a[half][:, t, :], ALU.mult, ALU.mult)
+
+        def part(tiles, u):
+            c0, w = UNITS[u]
+            return tiles[c0 // 256][:, :, c0 % 256 : c0 % 256 + w]
+
+        def square_a(u):
+            w = UNITS[u][1]
+            a2[u] = keep.tile([P, PACK, w], F32, name="a2%d" % u, tag="a2%d" % u)
+            nc.scalar.activation(a2[u][:], part(a, u), ACT.Square)
+
+        def denom(u):
+            w = UNITS[u][1]
+            den[u] = keep.tile([P, PACK, w], F32, name="den%d" % u)
+            nc.vector.tensor_tensor(den[u][:], a2[u][:], part(y2, u), ALU.add)
+
+        def invert(u):
+            w = UNITS[u][1]
+            r[u] = keep.tile([P, PACK, w], F32, name="r%d" % u, tag="r%d" % u, align_bytes=64)
+            r2[u] = keep.tile([P, PACK, w], F32, name="rr%d" % u)
+            nc.scalar.activation(r[u][:], den[u][:], ACT.Abs_reciprocal_sqrt, bias=0.25)
+            nc.scalar.activation(r2[u][:], r[u][:], ACT.Square)
+
+        def finish(u):
+            w = UNITS[u][1]
+            zb[u] = keep.tile([P, w, PACK], BF16, name="zb%d" % u, align_bytes=64)
+            nc.vector.tensor_tensor(zb[u][:].rearrange("p (c i) t -> p c t i", i=4), part(num, u).rearrange("p t (c i) -> p c t i", i=4),
+                                    r2[u][:].rearrange("p t (c i) -> p c t i", i=4), ALU.mult)
+
+        def quant(u):
+            c0, w = UNITS[u]
+            nc.vector.quantize_mx(out=zc[:, c0 : c0 + w].bitcast(FP8X4), scales=zs[:, c0 : c0 + w], in_=zb[u][:].rearrange("p c t -> p (c t)"))
+
+        def product(dst, t, c0, w):
+            cols = slice((t % 2) * P, (t % 2 + 1) * P)
+            nc.tensor.matmul_mx(out=dst, lhsT=w2c[t // 2][:, cols].bitcast(FP8X4), lhsT_scale=w2s[t // 2][:, cols],
+                                rhs=zc[:, c0 : c0 + w].bitcast(FP8X4), rhs_scale=zs[:, c0 : c0 + w], start=True, stop=True)
+
+        out_rows = out.rearrange("(p t) j -> p t j", t=PACK)
+        hs, c, e, up, neg, dn, res = [], [], [], [], [], [], []
+        for t in range(PACK):
+            hs.append(keep.tile([P, S], F32, name="hs%d" % t))
+            c.append(keep.tile([P, V], F32, name="c%d" % t))
+            e.append(keep.tile([P, V], F32, name="e%d" % t))
+            up.append(keep.tile([P, V], F32, name="up%d" % t))
+            neg.append(keep.tile([P, V], F32, name="neg%d" % t))
+            dn.append(keep.tile([P, V], F32, name="dn%d" % t))
+            res.append(keep.tile([P, S], F32, name="res%d" % t))
+
+        fetch(0, "a0")
+        square_y(0)
+        square_a(0)
+        numer(0)
+        denom(0)
+        square_y(1)
+        invert(0)
+        fetch(1, "a20")
+        square_a(1)
+        square_a(2)
+        numer(1)
+        denom(1)
+        denom(2)
+        lay_w2(0, "w2b0")
+        invert(1)
+        invert(2)
+        finish(0)
+        quant(0)
+        quant_w2(0)
+        product(hbank[0][:, 0:256], 0, 0, 256)
+        finish(1)
+        lay_w2(1, "r2")
+        finish(2)
+        quant(1)
+        product(hbank[0][:, 256:384], 0, 256, 128)
+        nc.scalar.copy(hs[0][:, 0:384], hbank[0][:, 0:384])
+        quant(2)
+        h0_last = psum.tile([P, 128], F32, name="h0_last", tag="ybank0")
+        product(h0_last[:], 0, 384, 128)
+        product(hbank[1][:], 1, 0, 512)
+        quant_w2(1)
+        nc.vector.tensor_copy(hs[0][:, 384:512], h0_last[:])
+        product(hbank[2][:], 2, 0, 512)
+        product(hbank[3][:], 3, 0, 512)
+        nc.scalar.copy(hs[1][:], hbank[1][:])
+
+        def pair(t):
+            nc.vector.tensor_copy(c[t][:], hs[t][:].indirect(la_sb[:]))
+            nc.vector.tensor_tensor(e[t][:], hs[t][:].indirect(lb_sb[:]), c[t][:], ALU.subtract)
+            nc.scalar.activation(up[t][:], e[t][:], ACT.Relu)
+            nc.scalar.activation(neg[t][:], e[t][:], ACT.Relu, scale=-1.0)
+            nc.scalar.activation(dn[t][:], neg[t][:], ACT.Copy, scale=-1.0)
+
+        def put_a(t):
+            nc.vector.tensor_tensor(res[t][:].indirect(la_sb[:]), c[t][:], up[t][:], ALU.add)
+
+        def put_b(t):
+            nc.vector.tensor_tensor(res[t][:].indirect(lb_sb[:]), c[t][:], dn[t][:], ALU.add)
+            nc.sync.dma_start(out_rows[:, t, :], res[t][:])
+
+        pair(0)
+        nc.scalar.copy(hs[2][:], hbank[2][:])
+        pair(1)
+        nc.scalar.copy(hs[3][:], hbank[3][:])
+        put_a(0)
+        pair(2)
+        put_b(0)
+        put_a(1)
+        pair(3)
+        put_b(1)
+        put_a(2)
+        put_a(3)
+        put_b(2)
+        put_b(3)

@@ -1,6 +1,7 @@
 from contextlib import ExitStack
 
 import concourse.mybir as mybir
+from concourse.masks import make_identity
 
 K, T, S, V, N, H = 512, 2048, 512, 256, 512, 512
 FLOPS = 2 * K * H * S + 2 * H * N * S
@@ -17,7 +18,9 @@ ACT = mybir.ActivationFunctionType
 
 P = 128
 PACK = 4
-UNITS = ((0, 256), (256, 128), (384, 128))
+HALF = S // 2
+QUARTER = P
+LIST_ROWS = 16
 
 
 def tile_picked_normord_none_p_kernel(tc, x_words, x_scales, w1, gn, w2, offs, n1, la, lb, out):
@@ -26,28 +29,31 @@ def tile_picked_normord_none_p_kernel(tc, x_words, x_scales, w1, gn, w2, offs, n
         lists = ctx.enter_context(tc.tile_pool(name="lists", bufs=1))
         keep = ctx.enter_context(tc.tile_pool(name="keep", bufs=1))
         psum = ctx.enter_context(tc.psum_pool(name="psum", bufs=1))
+        turn = ctx.enter_context(tc.psum_pool(name="turn", bufs=2))
 
-        offs_sb = lists.tile([P, S // 16], U16, name="offs_sb")
-        n1_sb = lists.tile([P, S // 16], U16, name="n1_sb")
-        la_sb = lists.tile([P, V // 16], U16, name="la_sb")
-        lb_sb = lists.tile([P, V // 16], U16, name="lb_sb")
+        offs_sb = lists.tile([P, S // LIST_ROWS], U16, name="offs_sb")
+        n1_sb = lists.tile([P, S // LIST_ROWS], U16, name="n1_sb")
+        la_sb = lists.tile([P, V // LIST_ROWS], U16, name="la_sb")
+        lb_sb = lists.tile([P, V // LIST_ROWS], U16, name="lb_sb")
 
-        xw = keep.tile([P, T], U32, name="xw", align_bytes=64)
-        xs = keep.tile([P, T], U8, name="xs", align_bytes=64)
-        nc.vector.memset(xs[:].bitcast(I32), 0)
+        x_words_sb = keep.tile([P, T], U32, name="x_words_sb", align_bytes=64)
+        x_scales_sb = keep.tile([P, T], U8, name="x_scales_sb", align_bytes=64)
+        nc.vector.memset(x_scales_sb[:].bitcast(I32), 0)
         one = keep.tile([P, 1], F32, name="one")
         nc.vector.memset(one[:], 1.0)
         warm = keep.tile([P, 1], F32, name="warm")
         nc.scalar.activation(warm[:], one[:], ACT.Abs_reciprocal_sqrt)
+        ident = keep.tile([P, P], F32, name="ident")
+        make_identity(nc, ident[:])
 
-        nc.sync.dma_start(xw[:].bitcast(I32), x_words[0].rearrange("p n t -> p (n t)").bitcast(I32))
-        for q in range(4):
-            nc.sync.dma_start(xs[32 * q : 32 * q + 4, :].bitcast(I32), x_scales[0, 4 * q : 4 * q + 4, :].bitcast(I32))
+        nc.sync.dma_start(x_words_sb[:].bitcast(I32), x_words[0].rearrange("p n t -> p (n t)").bitcast(I32))
+        for r in range(4):
+            nc.sync.dma_start(x_scales_sb[r:P:32, :].bitcast(I32), x_scales[0, r:16:4, :].bitcast(I32))
         nc.sync.dma_start(offs_sb[:], offs)
         w1_rows = w1.rearrange("(p j) c -> p j c", j=PACK)
-        w1_raw = [keep.tile([P, PACK, H // 2], F32, name="w1_raw%d" % u) for u in range(2)]
-        for u in range(2):
-            nc.sync.dma_start(w1_raw[u][:], w1_rows[:, :, u * 256 : (u + 1) * 256])
+        w1_raw = [keep.tile([P, PACK, H // 2], F32, name="w1_raw%d" % half) for half in range(2)]
+        for half in range(2):
+            nc.sync.dma_start(w1_raw[half][:], w1_rows[:, :, half * (H // 2) : (half + 1) * (H // 2)])
         nc.sync.dma_start(n1_sb[:], n1)
         gn_sb = keep.tile([P, PACK], F32, name="gn_sb")
         nc.sync.dma_start(gn_sb[:], gn.rearrange("(p t) o -> p (t o)", t=PACK))
@@ -56,173 +62,222 @@ def tile_picked_normord_none_p_kernel(tc, x_words, x_scales, w1, gn, w2, offs, n
         nc.sync.dma_start(la_sb[:], la)
         nc.sync.dma_start(lb_sb[:], lb)
 
-        gw = keep.tile([P, S], U32, name="gw", align_bytes=64)
-        gs = keep.tile([P, S], U8, name="gs", align_bytes=64)
-        nc.vector.tensor_copy(gw[:], xw[:].indirect(offs_sb[:]))
-        nc.vector.tensor_copy(gs[:], xs[:].indirect(offs_sb[:]))
+        picked_words = keep.tile([P, S], U32, name="picked_words", align_bytes=64)
+        picked_scales = keep.tile([P, S], U8, name="picked_scales", align_bytes=64)
+        nc.vector.tensor_copy(picked_words[:], x_words_sb[:].indirect(offs_sb[:]))
+        nc.vector.tensor_copy(picked_scales[:], x_scales_sb[:].indirect(offs_sb[:]))
 
-        w1b = keep.tile([P, PACK, P, PACK], BF16, name="w1b", align_bytes=64)
-        w1_dst = w1b[:].rearrange("p t m j -> p m j t")
+        w1_laid = [keep.tile([P, 2, P, PACK], BF16, name="w1_laid%d" % d, align_bytes=64) for d in range(2)]
+        w1_dst = [laid[:].rearrange("p t m j -> p m j t") for laid in w1_laid]
         w1_src = [raw[:].rearrange("p j (m t) -> p m j t", t=PACK) for raw in w1_raw]
-        nc.scalar.copy(w1_dst[:, 0:64], w1_src[0])
-        nc.vector.tensor_copy(w1_dst[:, 64:104], w1_src[1][:, 0:40])
-        nc.scalar.copy(w1_dst[:, 104:128], w1_src[1][:, 40:64])
+        nc.scalar.copy(w1_dst[0][:, : P // 2], w1_src[0][:, :, :, 0:2])
+        nc.scalar.copy(w1_dst[1][:, : P // 2], w1_src[0][:, :, :, 2:4])
+        nc.vector.tensor_copy(w1_dst[0][:, P // 2 :], w1_src[1][:, :, :, 0:2])
+        nc.scalar.copy(w1_dst[1][:, P // 2 :], w1_src[1][:, :, :, 2:4])
 
-        w1c = keep.tile([P, H], U32, name="w1c", align_bytes=64)
-        w1s = keep.tile([P, H], U8, name="w1s", align_bytes=64)
-        ybank = [psum.tile([P, S], F32, name="ybank%d" % t, tag="ybank%d" % t) for t in range(PACK)]
+        w1_words = keep.tile([P, H], U32, name="w1_words", align_bytes=64)
+        w1_scales = keep.tile([P, H], U8, name="w1_scales", align_bytes=64)
+        y_bank = [psum.tile([P, S], F32, name="y_bank%d" % t, tag="rows%d" % t) for t in range(PACK)]
         for t in range(PACK):
             cols = slice(t * P, (t + 1) * P)
-            nc.vector.quantize_mx(out=w1c[:, cols].bitcast(FP8X4), scales=w1s[:, cols], in_=w1b[:, t].rearrange("p m j -> p (m j)"))
+            nc.vector.quantize_mx(out=w1_words[:, cols].bitcast(FP8X4), scales=w1_scales[:, cols], in_=w1_laid[t // 2][:, t % 2].rearrange("p m j -> p (m j)"))
         for t in range(PACK):
             cols = slice(t * P, (t + 1) * P)
-            nc.tensor.matmul_mx(out=ybank[t][:], lhsT=w1c[:, cols].bitcast(FP8X4), lhsT_scale=w1s[:, cols],
-                                rhs=gw[:].bitcast(FP8X4), rhs_scale=gs[:], start=True, stop=True)
-        ys = [keep.tile([P, S], F32, name="ys%d" % t) for t in range(PACK)]
-        nc.vector.tensor_copy(ys[0][:], ybank[0][:])
+            nc.tensor.matmul_mx(
+                out=y_bank[t][:],
+                lhsT=w1_words[:, cols].bitcast(FP8X4),
+                lhsT_scale=w1_scales[:, cols],
+                rhs=picked_words[:].bitcast(FP8X4),
+                rhs_scale=picked_scales[:],
+                start=True,
+                stop=True,
+            )
+        y = [keep.tile([P, S], F32, name="y%d" % t) for t in range(PACK)]
+        nc.vector.tensor_copy(y[0][:], y_bank[0][:])
         for t in range(1, PACK):
-            nc.scalar.copy(ys[t][:], ybank[t][:])
-        y2 = [keep.tile([P, PACK, S // 2], F32, name="y2%d" % u) for u in range(2)]
+            nc.scalar.copy(y[t][:], y_bank[t][:])
 
-        def square_y(half):
-            for t in range(PACK):
-                nc.scalar.activation(y2[half][:, t, :], ybank[t][:, half * 256 : (half + 1) * 256], ACT.Square)
-
-        w2c = [keep.tile([P, 2 * P], U32, name="w2c%d" % u, align_bytes=64) for u in range(2)]
-        w2s = [keep.tile([P, 2 * P], U8, name="w2s%d" % u, align_bytes=64) for u in range(2)]
         w2_src = w2_raw[:].rearrange("p j (m t) -> p m j t", t=PACK)
-        w2b = {}
+        w2_words = [keep.tile([P, 2 * P], U32, name="w2_words%d" % d, align_bytes=64) for d in range(2)]
+        w2_scales = [keep.tile([P, 2 * P], U8, name="w2_scales%d" % d, align_bytes=64) for d in range(2)]
+        z_words = keep.tile([P, S], U32, name="z_words", align_bytes=64)
+        z_scales = keep.tile([P, S], U8, name="z_scales", align_bytes=64)
+        w2_laid, a, num, a_sq, den, root, inv, z_laid = {}, {}, {}, {}, {}, {}, {}, {}
 
-        def lay_w2(u, tag):
-            w2b[u] = keep.tile([P, 2, P, PACK], BF16, name="w2b%d" % u, tag=tag, align_bytes=64)
-            nc.scalar.copy(w2b[u][:].rearrange("p t m j -> p m j t"), w2_src[:, :, :, 2 * u : 2 * u + 2])
+        def lay_w2(d, tag):
+            w2_laid[d] = keep.tile([P, 2, P, PACK], BF16, name="w2_laid%d" % d, tag=tag, align_bytes=64)
+            nc.scalar.copy(w2_laid[d][:].rearrange("p t m j -> p m j t"), w2_src[:, :, :, 2 * d : 2 * d + 2])
 
-        def quant_w2(u):
-            nc.vector.quantize_mx(out=w2c[u][:].bitcast(FP8X4), scales=w2s[u][:], in_=w2b[u][:].rearrange("p t m j -> p (t m j)"))
+        def quantise_w2(d):
+            nc.vector.quantize_mx(out=w2_words[d][:].bitcast(FP8X4), scales=w2_scales[d][:], in_=w2_laid[d][:].rearrange("p t m j -> p (t m j)"))
 
-        hbank = [psum.tile([P, S], F32, name="hbank%d" % t) for t in range(PACK)]
-        zc = keep.tile([P, S], U32, name="zc", align_bytes=64)
-        zs = keep.tile([P, S], U8, name="zs", align_bytes=64)
-        a, num, a2, den, r, r2, zb = {}, {}, {}, {}, {}, {}, {}
+        def square_y(dst, t, half):
+            y_half = y[t][:, half * HALF : (half + 1) * HALF]
+            nc.gpsimd.tensor_tensor(dst, y_half, y_half, ALU.mult)
 
-        def fetch(half, tag):
-            a[half] = keep.tile([P, PACK, 256], F32, name="a%d" % half, tag=tag)
+        def gather_a(half):
+            offsets = n1_sb[:, half * HALF // LIST_ROWS : (half + 1) * HALF // LIST_ROWS]
             for t in range(PACK):
-                nc.vector.tensor_copy(a[half][:, t, :], ys[t][:].indirect(n1_sb[:, half * 16 : (half + 1) * 16]))
+                nc.vector.tensor_copy(a[half][:, t, :], y[t][:].indirect(offsets))
 
-        def numer(half):
-            num[half] = keep.tile([P, PACK, 256], F32, name="num%d" % half)
+        def numerators(half):
             for t in range(PACK):
-                nc.vector.scalar_tensor_tensor(num[half][:, t, :], ybank[t][:, half * 256 : (half + 1) * 256], gn_sb[:, t : t + 1], a[half][:, t, :], ALU.mult, ALU.mult)
+                y_half = y_bank[t][:, half * HALF : (half + 1) * HALF]
+                nc.vector.scalar_tensor_tensor(num[half][:, t, :], y_half, gn_sb[:, t : t + 1], a[half][:, t, :], ALU.mult, ALU.mult)
 
-        def part(tiles, u):
-            c0, w = UNITS[u]
-            return tiles[c0 // 256][:, :, c0 % 256 : c0 % 256 + w]
+        def quarter_of(half_tile, q):
+            return half_tile[:, :, (q % 2) * QUARTER : (q % 2 + 1) * QUARTER]
 
-        def square_a(u):
-            w = UNITS[u][1]
-            a2[u] = keep.tile([P, PACK, w], F32, name="a2%d" % u, tag="a2%d" % u)
-            nc.scalar.activation(a2[u][:], part(a, u), ACT.Square)
+        def square_a(q):
+            a_sq[q] = keep.tile([P, PACK, QUARTER], F32, name="a_sq%d" % q, tag="a_sq", bufs=2)
+            nc.scalar.activation(a_sq[q][:], quarter_of(a[q // 2], q), ACT.Square)
 
-        def denom(u):
-            w = UNITS[u][1]
-            den[u] = keep.tile([P, PACK, w], F32, name="den%d" % u)
-            nc.vector.tensor_tensor(den[u][:], a2[u][:], part(y2, u), ALU.add)
+        def sum_by_transposes(q):
+            den[q] = turn.tile([P, PACK, P], F32, name="den%d" % q, tag="turned")
+            for t in range(PACK):
+                nc.tensor.matmul(den[q][:, t, :], y_sq_first[t][:, q * QUARTER : (q + 1) * QUARTER], ident[:], is_transpose=True, start=(t == 0), stop=False)
+            for t in range(PACK):
+                nc.tensor.matmul(den[q][:, t, :], a_sq[q][:, t, :], ident[:], is_transpose=True, start=False, stop=(t == PACK - 1))
 
-        def invert(u):
-            w = UNITS[u][1]
-            r[u] = keep.tile([P, PACK, w], F32, name="r%d" % u, tag="r%d" % u, align_bytes=64)
-            r2[u] = keep.tile([P, PACK, w], F32, name="rr%d" % u)
-            nc.scalar.activation(r[u][:], den[u][:], ACT.Abs_reciprocal_sqrt, bias=0.25)
-            nc.scalar.activation(r2[u][:], r[u][:], ACT.Square)
+        def sum_on_gpsimd(q):
+            den[q] = keep.tile([P, PACK, QUARTER], F32, name="den%d" % q)
+            nc.gpsimd.tensor_tensor(den[q][:], a_sq[q][:], quarter_of(y_sq_second, q), ALU.add)
 
-        def finish(u):
-            w = UNITS[u][1]
-            zb[u] = keep.tile([P, w, PACK], BF16, name="zb%d" % u, align_bytes=64)
-            nc.vector.tensor_tensor(zb[u][:].rearrange("p (c i) t -> p c t i", i=4), part(num, u).rearrange("p t (c i) -> p c t i", i=4),
-                                    r2[u][:].rearrange("p t (c i) -> p c t i", i=4), ALU.mult)
+        def inverse_root(q):
+            root[q] = keep.tile([P, PACK, QUARTER], F32, name="root%d" % q, tag="root%d" % q, align_bytes=64)
+            nc.scalar.activation(root[q][:], den[q][:], ACT.Abs_reciprocal_sqrt, bias=0.25)
 
-        def quant(u):
-            c0, w = UNITS[u]
-            nc.vector.quantize_mx(out=zc[:, c0 : c0 + w].bitcast(FP8X4), scales=zs[:, c0 : c0 + w], in_=zb[u][:].rearrange("p c t -> p (c t)"))
+        def invert(q):
+            inv[q] = keep.tile([P, PACK, QUARTER], F32, name="inv%d" % q)
+            nc.scalar.activation(inv[q][:], root[q][:], ACT.Square)
 
-        def product(dst, t, c0, w):
+        def turn_back(q):
+            turned = inv[q]
+            inv[q] = turn.tile([P, PACK, P], F32, name="inv_back%d" % q, tag="back")
+            for t in range(PACK):
+                nc.tensor.transpose(inv[q][:, t, :], turned[:, t, :], ident[:])
+
+        def finish_z(q):
+            z_laid[q] = keep.tile([P, QUARTER, PACK], BF16, name="z_laid%d" % q, align_bytes=64)
+            nc.vector.tensor_tensor(
+                z_laid[q][:].rearrange("p (c i) t -> p c t i", i=2),
+                inv[q][:].rearrange("p t (c i) -> p c t i", i=2),
+                quarter_of(num[q // 2], q).rearrange("p t (c i) -> p c t i", i=2),
+                ALU.mult,
+            )
+
+        def quantise_z(q):
+            cols = slice(q * QUARTER, (q + 1) * QUARTER)
+            nc.vector.quantize_mx(out=z_words[:, cols].bitcast(FP8X4), scales=z_scales[:, cols], in_=z_laid[q][:].rearrange("p c t -> p (c t)"))
+
+        y_sq_first = [keep.tile([P, HALF], F32, name="y_sq_first%d" % t, tag="y_sq%d" % t, align_bytes=64) for t in range(PACK)]
+        for t in range(PACK):
+            square_y(y_sq_first[t][:], t, 0)
+        a_first = keep.tile([P, PACK, HALF], F32, name="a_first")
+        a[0] = a_first[:]
+        gather_a(0)
+        lay_w2(0, "w2_laid0")
+        square_a(0)
+        square_a(1)
+        sum_by_transposes(0)
+        sum_by_transposes(1)
+        y_sq_second = keep.tile([P, PACK, HALF], F32, name="y_sq_second", tag="y_sq3", align_bytes=64)
+        for t in range(PACK):
+            square_y(y_sq_second[:, t, :], t, 1)
+        quantise_w2(0)
+        a_second_num_first = keep.tile([P, 2, PACK, HALF], F32, name="a_second_num_first", tag="y_sq2", align_bytes=64)
+        a[1] = a_second_num_first[:, 0]
+        num[0] = a_second_num_first[:, 1]
+        gather_a(1)
+        inverse_root(0)
+        inverse_root(1)
+        square_a(2)
+        invert(0)
+        turn_back(0)
+        square_a(3)
+        numerators(0)
+        sum_on_gpsimd(2)
+        sum_on_gpsimd(3)
+        invert(1)
+        turn_back(1)
+        num_second = keep.tile([P, PACK, HALF], F32, name="num_second")
+        num[1] = num_second[:]
+        numerators(1)
+        inverse_root(2)
+        inverse_root(3)
+        invert(2)
+        invert(3)
+        finish_z(0)
+        finish_z(1)
+        quantise_z(0)
+        quantise_z(1)
+        finish_z(2)
+        finish_z(3)
+        quantise_z(2)
+
+        def product_h(dst, t, first, width):
             cols = slice((t % 2) * P, (t % 2 + 1) * P)
-            nc.tensor.matmul_mx(out=dst, lhsT=w2c[t // 2][:, cols].bitcast(FP8X4), lhsT_scale=w2s[t // 2][:, cols],
-                                rhs=zc[:, c0 : c0 + w].bitcast(FP8X4), rhs_scale=zs[:, c0 : c0 + w], start=True, stop=True)
+            tokens = slice(first, first + width)
+            nc.tensor.matmul_mx(
+                out=dst,
+                lhsT=w2_words[t // 2][:, cols].bitcast(FP8X4),
+                lhsT_scale=w2_scales[t // 2][:, cols],
+                rhs=z_words[:, tokens].bitcast(FP8X4),
+                rhs_scale=z_scales[:, tokens],
+                start=True,
+                stop=True,
+            )
+
+        h_bank = [psum.tile([P, S], F32, name="h_bank%d" % t, tag="rows%d" % t) for t in range(PACK)]
+        h = [keep.tile([P, S], F32, name="h%d" % t) for t in range(PACK)]
+        last = S - QUARTER
+        product_h(h_bank[0][:, :HALF], 0, 0, HALF)
+        product_h(h_bank[0][:, HALF:last], 0, HALF, QUARTER)
+        nc.scalar.copy(h[0][:, :last], h_bank[0][:, :last])
+        lay_w2(1, "root3")
+        quantise_z(3)
+        h0_last = turn.tile([P, QUARTER], F32, name="h0_last", tag="turned")
+        product_h(h0_last[:], 0, last, QUARTER)
+        product_h(h_bank[1][:], 1, 0, S)
+        nc.vector.tensor_copy(h[0][:, last:], h0_last[:])
+        quantise_w2(1)
+        product_h(h_bank[2][:], 2, 0, S)
+        product_h(h_bank[3][:], 3, 0, S)
+        nc.scalar.copy(h[1][:], h_bank[1][:])
 
         out_rows = out.rearrange("(p t) j -> p t j", t=PACK)
-        hs, c, e, up, neg, dn, res = [], [], [], [], [], [], []
-        for t in range(PACK):
-            hs.append(keep.tile([P, S], F32, name="hs%d" % t))
-            c.append(keep.tile([P, V], F32, name="c%d" % t))
-            e.append(keep.tile([P, V], F32, name="e%d" % t))
-            up.append(keep.tile([P, V], F32, name="up%d" % t))
-            neg.append(keep.tile([P, V], F32, name="neg%d" % t))
-            dn.append(keep.tile([P, V], F32, name="dn%d" % t))
-            res.append(keep.tile([P, S], F32, name="res%d" % t))
+        c = [keep.tile([P, V], F32, name="c%d" % t) for t in range(PACK)]
+        rise = [keep.tile([P, V], F32, name="rise%d" % t) for t in range(PACK)]
+        fall = [keep.tile([P, V], F32, name="fall%d" % t) for t in range(PACK)]
+        result = [keep.tile([P, S], F32, name="result%d" % t) for t in range(PACK)]
 
-        fetch(0, "a0")
-        square_y(0)
-        square_a(0)
-        numer(0)
-        denom(0)
-        square_y(1)
-        invert(0)
-        fetch(1, "a20")
-        square_a(1)
-        square_a(2)
-        numer(1)
-        denom(1)
-        denom(2)
-        lay_w2(0, "w2b0")
-        invert(1)
-        invert(2)
-        finish(0)
-        quant(0)
-        quant_w2(0)
-        product(hbank[0][:, 0:256], 0, 0, 256)
-        finish(1)
-        lay_w2(1, "r2")
-        finish(2)
-        quant(1)
-        product(hbank[0][:, 256:384], 0, 256, 128)
-        nc.scalar.copy(hs[0][:, 0:384], hbank[0][:, 0:384])
-        quant(2)
-        h0_last = psum.tile([P, 128], F32, name="h0_last", tag="ybank0")
-        product(h0_last[:], 0, 384, 128)
-        product(hbank[1][:], 1, 0, 512)
-        quant_w2(1)
-        nc.vector.tensor_copy(hs[0][:, 384:512], h0_last[:])
-        product(hbank[2][:], 2, 0, 512)
-        product(hbank[3][:], 3, 0, 512)
-        nc.scalar.copy(hs[1][:], hbank[1][:])
+        def gather_pairs(t):
+            gap = keep.tile([P, V], F32, name="gap%d" % t)
+            drop = keep.tile([P, V], F32, name="drop%d" % t)
+            nc.vector.tensor_copy(c[t][:], h[t][:].indirect(la_sb[:]))
+            nc.vector.tensor_tensor(gap[:], h[t][:].indirect(lb_sb[:]), c[t][:], ALU.subtract)
+            nc.scalar.activation(rise[t][:], gap[:], ACT.Relu)
+            nc.scalar.activation(drop[:], gap[:], ACT.Relu, scale=-1.0)
+            nc.scalar.activation(fall[t][:], drop[:], ACT.Copy, scale=-1.0)
 
-        def pair(t):
-            nc.vector.tensor_copy(c[t][:], hs[t][:].indirect(la_sb[:]))
-            nc.vector.tensor_tensor(e[t][:], hs[t][:].indirect(lb_sb[:]), c[t][:], ALU.subtract)
-            nc.scalar.activation(up[t][:], e[t][:], ACT.Relu)
-            nc.scalar.activation(neg[t][:], e[t][:], ACT.Relu, scale=-1.0)
-            nc.scalar.activation(dn[t][:], neg[t][:], ACT.Copy, scale=-1.0)
+        def put_larger(t):
+            nc.vector.tensor_tensor(result[t][:].indirect(la_sb[:]), c[t][:], rise[t][:], ALU.add)
 
-        def put_a(t):
-            nc.vector.tensor_tensor(res[t][:].indirect(la_sb[:]), c[t][:], up[t][:], ALU.add)
+        def put_smaller_and_store(t):
+            nc.vector.tensor_tensor(result[t][:].indirect(lb_sb[:]), c[t][:], fall[t][:], ALU.add)
+            nc.sync.dma_start(out_rows[:, t, :], result[t][:])
 
-        def put_b(t):
-            nc.vector.tensor_tensor(res[t][:].indirect(lb_sb[:]), c[t][:], dn[t][:], ALU.add)
-            nc.sync.dma_start(out_rows[:, t, :], res[t][:])
-
-        pair(0)
-        nc.scalar.copy(hs[2][:], hbank[2][:])
-        pair(1)
-        nc.scalar.copy(hs[3][:], hbank[3][:])
-        put_a(0)
-        pair(2)
-        put_b(0)
-        put_a(1)
-        pair(3)
-        put_b(1)
-        put_a(2)
-        put_a(3)
-        put_b(2)
-        put_b(3)
+        gather_pairs(0)
+        nc.scalar.copy(h[2][:], h_bank[2][:])
+        gather_pairs(1)
+        nc.scalar.copy(h[3][:], h_bank[3][:])
+        put_larger(0)
+        gather_pairs(2)
+        put_smaller_and_store(0)
+        put_larger(1)
+        gather_pairs(3)
+        put_smaller_and_store(1)
+        put_larger(2)
+        put_larger(3)
+        put_smaller_and_store(2)
+        put_smaller_and_store(3)

from contextlib import ExitStack

import concourse.mybir as mybir
from concourse.masks import make_identity

K, T, S, V, N, H = 512, 2048, 512, 256, 512, 512
FLOPS = 2 * K * H * S + 2 * H * N * S

F32 = mybir.dt.float32
BF16 = mybir.dt.bfloat16
I32 = mybir.dt.int32
U32 = mybir.dt.uint32
U16 = mybir.dt.uint16
U8 = mybir.dt.uint8
FP8X4 = mybir.dt.float8_e4m3fn_x4
ALU = mybir.AluOpType
ACT = mybir.ActivationFunctionType

P = 128
PACK = 4
HALF = S // 2
QUARTER = P
LIST_ROWS = 16


def tile_picked_normord_none_p_kernel(tc, x_words, x_scales, w1, gn, w2, offs, n1, la, lb, out):
    nc = tc.nc
    with ExitStack() as ctx:
        lists = ctx.enter_context(tc.tile_pool(name="lists", bufs=1))
        keep = ctx.enter_context(tc.tile_pool(name="keep", bufs=1))
        psum = ctx.enter_context(tc.psum_pool(name="psum", bufs=1))
        turn = ctx.enter_context(tc.psum_pool(name="turn", bufs=2))

        offs_sb = lists.tile([P, S // LIST_ROWS], U16, name="offs_sb")
        n1_sb = lists.tile([P, S // LIST_ROWS], U16, name="n1_sb")
        la_sb = lists.tile([P, V // LIST_ROWS], U16, name="la_sb")
        lb_sb = lists.tile([P, V // LIST_ROWS], U16, name="lb_sb")

        x_words_sb = keep.tile([P, T], U32, name="x_words_sb", align_bytes=64)
        x_scales_sb = keep.tile([P, T], U8, name="x_scales_sb", align_bytes=64)
        nc.vector.memset(x_scales_sb[:].bitcast(I32), 0)
        one = keep.tile([P, 1], F32, name="one")
        nc.vector.memset(one[:], 1.0)
        warm = keep.tile([P, 1], F32, name="warm")
        nc.scalar.activation(warm[:], one[:], ACT.Abs_reciprocal_sqrt)
        ident = keep.tile([P, P], F32, name="ident")
        make_identity(nc, ident[:])

        nc.sync.dma_start(x_words_sb[:].bitcast(I32), x_words[0].rearrange("p n t -> p (n t)").bitcast(I32))
        for r in range(4):
            nc.sync.dma_start(x_scales_sb[r:P:32, :].bitcast(I32), x_scales[0, r:16:4, :].bitcast(I32))
        nc.sync.dma_start(offs_sb[:], offs)
        w1_rows = w1.rearrange("(p j) c -> p j c", j=PACK)
        w1_raw = [keep.tile([P, PACK, H // 2], F32, name="w1_raw%d" % half) for half in range(2)]
        for half in range(2):
            nc.sync.dma_start(w1_raw[half][:], w1_rows[:, :, half * (H // 2) : (half + 1) * (H // 2)])
        nc.sync.dma_start(n1_sb[:], n1)
        gn_sb = keep.tile([P, PACK], F32, name="gn_sb")
        nc.sync.dma_start(gn_sb[:], gn.rearrange("(p t) o -> p (t o)", t=PACK))
        w2_raw = keep.tile([P, PACK, N], F32, name="w2_raw")
        nc.sync.dma_start(w2_raw[:], w2.rearrange("(p j) c -> p j c", j=PACK))
        nc.sync.dma_start(la_sb[:], la)
        nc.sync.dma_start(lb_sb[:], lb)

        picked_words = keep.tile([P, S], U32, name="picked_words", align_bytes=64)
        picked_scales = keep.tile([P, S], U8, name="picked_scales", align_bytes=64)
        nc.vector.tensor_copy(picked_words[:], x_words_sb[:].indirect(offs_sb[:]))
        nc.vector.tensor_copy(picked_scales[:], x_scales_sb[:].indirect(offs_sb[:]))

        w1_laid = [keep.tile([P, 2, P, PACK], BF16, name="w1_laid%d" % d, align_bytes=64) for d in range(2)]
        w1_dst = [laid[:].rearrange("p t m j -> p m j t") for laid in w1_laid]
        w1_src = [raw[:].rearrange("p j (m t) -> p m j t", t=PACK) for raw in w1_raw]
        nc.scalar.copy(w1_dst[0][:, : P // 2], w1_src[0][:, :, :, 0:2])
        nc.scalar.copy(w1_dst[1][:, : P // 2], w1_src[0][:, :, :, 2:4])
        nc.vector.tensor_copy(w1_dst[0][:, P // 2 :], w1_src[1][:, :, :, 0:2])
        nc.scalar.copy(w1_dst[1][:, P // 2 :], w1_src[1][:, :, :, 2:4])

        w1_words = keep.tile([P, H], U32, name="w1_words", align_bytes=64)
        w1_scales = keep.tile([P, H], U8, name="w1_scales", align_bytes=64)
        y_bank = [psum.tile([P, S], F32, name="y_bank%d" % t, tag="rows%d" % t) for t in range(PACK)]
        for t in range(PACK):
            cols = slice(t * P, (t + 1) * P)
            nc.vector.quantize_mx(out=w1_words[:, cols].bitcast(FP8X4), scales=w1_scales[:, cols], in_=w1_laid[t // 2][:, t % 2].rearrange("p m j -> p (m j)"))
        for t in range(PACK):
            cols = slice(t * P, (t + 1) * P)
            nc.tensor.matmul_mx(
                out=y_bank[t][:],
                lhsT=w1_words[:, cols].bitcast(FP8X4),
                lhsT_scale=w1_scales[:, cols],
                rhs=picked_words[:].bitcast(FP8X4),
                rhs_scale=picked_scales[:],
                start=True,
                stop=True,
            )
        y = [keep.tile([P, S], F32, name="y%d" % t) for t in range(PACK)]
        nc.vector.tensor_copy(y[0][:], y_bank[0][:])
        for t in range(1, PACK):
            nc.scalar.copy(y[t][:], y_bank[t][:])

        w2_src = w2_raw[:].rearrange("p j (m t) -> p m j t", t=PACK)
        w2_words = [keep.tile([P, 2 * P], U32, name="w2_words%d" % d, align_bytes=64) for d in range(2)]
        w2_scales = [keep.tile([P, 2 * P], U8, name="w2_scales%d" % d, align_bytes=64) for d in range(2)]
        z_words = keep.tile([P, S], U32, name="z_words", align_bytes=64)
        z_scales = keep.tile([P, S], U8, name="z_scales", align_bytes=64)
        w2_laid, a, num, a_sq, den, root, inv, z_laid = {}, {}, {}, {}, {}, {}, {}, {}

        def lay_w2(d, tag):
            w2_laid[d] = keep.tile([P, 2, P, PACK], BF16, name="w2_laid%d" % d, tag=tag, align_bytes=64)
            nc.scalar.copy(w2_laid[d][:].rearrange("p t m j -> p m j t"), w2_src[:, :, :, 2 * d : 2 * d + 2])

        def quantise_w2(d):
            nc.vector.quantize_mx(out=w2_words[d][:].bitcast(FP8X4), scales=w2_scales[d][:], in_=w2_laid[d][:].rearrange("p t m j -> p (t m j)"))

        def square_y(dst, t, half):
            y_half = y[t][:, half * HALF : (half + 1) * HALF]
            nc.gpsimd.tensor_tensor(dst, y_half, y_half, ALU.mult)

        def gather_a(half):
            offsets = n1_sb[:, half * HALF // LIST_ROWS : (half + 1) * HALF // LIST_ROWS]
            for t in range(PACK):
                nc.vector.tensor_copy(a[half][:, t, :], y[t][:].indirect(offsets))

        def numerators(half):
            for t in range(PACK):
                y_half = y_bank[t][:, half * HALF : (half + 1) * HALF]
                nc.vector.scalar_tensor_tensor(num[half][:, t, :], y_half, gn_sb[:, t : t + 1], a[half][:, t, :], ALU.mult, ALU.mult)

        def quarter_of(half_tile, q):
            return half_tile[:, :, (q % 2) * QUARTER : (q % 2 + 1) * QUARTER]

        def square_a(q):
            a_sq[q] = keep.tile([P, PACK, QUARTER], F32, name="a_sq%d" % q, tag="a_sq", bufs=2)
            nc.scalar.activation(a_sq[q][:], quarter_of(a[q // 2], q), ACT.Square)

        def sum_by_transposes(q):
            den[q] = turn.tile([P, PACK, P], F32, name="den%d" % q, tag="turned")
            for t in range(PACK):
                nc.tensor.matmul(den[q][:, t, :], y_sq_first[t][:, q * QUARTER : (q + 1) * QUARTER], ident[:], is_transpose=True, start=(t == 0), stop=False)
            for t in range(PACK):
                nc.tensor.matmul(den[q][:, t, :], a_sq[q][:, t, :], ident[:], is_transpose=True, start=False, stop=(t == PACK - 1))

        def sum_on_gpsimd(q):
            den[q] = keep.tile([P, PACK, QUARTER], F32, name="den%d" % q)
            nc.gpsimd.tensor_tensor(den[q][:], a_sq[q][:], quarter_of(y_sq_second, q), ALU.add)

        def inverse_root(q):
            root[q] = keep.tile([P, PACK, QUARTER], F32, name="root%d" % q, tag="root%d" % q, align_bytes=64)
            nc.scalar.activation(root[q][:], den[q][:], ACT.Abs_reciprocal_sqrt, bias=0.25)

        def invert(q):
            inv[q] = keep.tile([P, PACK, QUARTER], F32, name="inv%d" % q)
            nc.scalar.activation(inv[q][:], root[q][:], ACT.Square)

        def turn_back(q):
            turned = inv[q]
            inv[q] = turn.tile([P, PACK, P], F32, name="inv_back%d" % q, tag="back")
            for t in range(PACK):
                nc.tensor.transpose(inv[q][:, t, :], turned[:, t, :], ident[:])

        def finish_z(q):
            z_laid[q] = keep.tile([P, QUARTER, PACK], BF16, name="z_laid%d" % q, align_bytes=64)
            nc.vector.tensor_tensor(
                z_laid[q][:].rearrange("p (c i) t -> p c t i", i=2),
                inv[q][:].rearrange("p t (c i) -> p c t i", i=2),
                quarter_of(num[q // 2], q).rearrange("p t (c i) -> p c t i", i=2),
                ALU.mult,
            )

        def quantise_z(q):
            cols = slice(q * QUARTER, (q + 1) * QUARTER)
            nc.vector.quantize_mx(out=z_words[:, cols].bitcast(FP8X4), scales=z_scales[:, cols], in_=z_laid[q][:].rearrange("p c t -> p (c t)"))

        y_sq_first = [keep.tile([P, HALF], F32, name="y_sq_first%d" % t, tag="y_sq%d" % t, align_bytes=64) for t in range(PACK)]
        for t in range(PACK):
            square_y(y_sq_first[t][:], t, 0)
        a_first = keep.tile([P, PACK, HALF], F32, name="a_first")
        a[0] = a_first[:]
        gather_a(0)
        lay_w2(0, "w2_laid0")
        square_a(0)
        square_a(1)
        sum_by_transposes(0)
        sum_by_transposes(1)
        y_sq_second = keep.tile([P, PACK, HALF], F32, name="y_sq_second", tag="y_sq3", align_bytes=64)
        for t in range(PACK):
            square_y(y_sq_second[:, t, :], t, 1)
        quantise_w2(0)
        a_second_num_first = keep.tile([P, 2, PACK, HALF], F32, name="a_second_num_first", tag="y_sq2", align_bytes=64)
        a[1] = a_second_num_first[:, 0]
        num[0] = a_second_num_first[:, 1]
        gather_a(1)
        inverse_root(0)
        inverse_root(1)
        square_a(2)
        invert(0)
        turn_back(0)
        square_a(3)
        numerators(0)
        sum_on_gpsimd(2)
        sum_on_gpsimd(3)
        invert(1)
        turn_back(1)
        num_second = keep.tile([P, PACK, HALF], F32, name="num_second")
        num[1] = num_second[:]
        numerators(1)
        inverse_root(2)
        inverse_root(3)
        invert(2)
        invert(3)
        finish_z(0)
        finish_z(1)
        quantise_z(0)
        quantise_z(1)
        finish_z(2)
        finish_z(3)
        quantise_z(2)

        def product_h(dst, t, first, width):
            cols = slice((t % 2) * P, (t % 2 + 1) * P)
            tokens = slice(first, first + width)
            nc.tensor.matmul_mx(
                out=dst,
                lhsT=w2_words[t // 2][:, cols].bitcast(FP8X4),
                lhsT_scale=w2_scales[t // 2][:, cols],
                rhs=z_words[:, tokens].bitcast(FP8X4),
                rhs_scale=z_scales[:, tokens],
                start=True,
                stop=True,
            )

        h_bank = [psum.tile([P, S], F32, name="h_bank%d" % t, tag="rows%d" % t) for t in range(PACK)]
        h = [keep.tile([P, S], F32, name="h%d" % t) for t in range(PACK)]
        last = S - QUARTER
        product_h(h_bank[0][:, :HALF], 0, 0, HALF)
        product_h(h_bank[0][:, HALF:last], 0, HALF, QUARTER)
        nc.scalar.copy(h[0][:, :last], h_bank[0][:, :last])
        lay_w2(1, "root3")
        quantise_z(3)
        h0_last = turn.tile([P, QUARTER], F32, name="h0_last", tag="turned")
        product_h(h0_last[:], 0, last, QUARTER)
        product_h(h_bank[1][:], 1, 0, S)
        nc.vector.tensor_copy(h[0][:, last:], h0_last[:])
        quantise_w2(1)
        product_h(h_bank[2][:], 2, 0, S)
        product_h(h_bank[3][:], 3, 0, S)
        nc.scalar.copy(h[1][:], h_bank[1][:])

        out_rows = out.rearrange("(p t) j -> p t j", t=PACK)
        c = [keep.tile([P, V], F32, name="c%d" % t) for t in range(PACK)]
        rise = [keep.tile([P, V], F32, name="rise%d" % t) for t in range(PACK)]
        fall = [keep.tile([P, V], F32, name="fall%d" % t) for t in range(PACK)]
        result = [keep.tile([P, S], F32, name="result%d" % t) for t in range(PACK)]

        def gather_pairs(t):
            gap = keep.tile([P, V], F32, name="gap%d" % t)
            drop = keep.tile([P, V], F32, name="drop%d" % t)
            nc.vector.tensor_copy(c[t][:], h[t][:].indirect(la_sb[:]))
            nc.vector.tensor_tensor(gap[:], h[t][:].indirect(lb_sb[:]), c[t][:], ALU.subtract)
            nc.scalar.activation(rise[t][:], gap[:], ACT.Relu)
            nc.scalar.activation(drop[:], gap[:], ACT.Relu, scale=-1.0)
            nc.scalar.activation(fall[t][:], drop[:], ACT.Copy, scale=-1.0)

        def put_larger(t):
            nc.vector.tensor_tensor(result[t][:].indirect(la_sb[:]), c[t][:], rise[t][:], ALU.add)

        def put_smaller_and_store(t):
            nc.vector.tensor_tensor(result[t][:].indirect(lb_sb[:]), c[t][:], fall[t][:], ALU.add)
            nc.sync.dma_start(out_rows[:, t, :], result[t][:])

        gather_pairs(0)
        nc.scalar.copy(h[2][:], h_bank[2][:])
        gather_pairs(1)
        nc.scalar.copy(h[3][:], h_bank[3][:])
        put_larger(0)
        gather_pairs(2)
        put_smaller_and_store(0)
        put_larger(1)
        gather_pairs(3)
        put_smaller_and_store(1)
        put_larger(2)
        put_larger(3)
        put_smaller_and_store(2)
        put_smaller_and_store(3)
